import numpy as np
import ml_dtypes


def mxq(x, axis, fmt="e4m3"):
    dtype, down = {"e4m3": (ml_dtypes.float8_e4m3fn, 7), "e5m2": (ml_dtypes.float8_e5m2, 14)}[fmt]
    v = np.moveaxis(np.asarray(x, np.float32).astype(ml_dtypes.bfloat16).astype(np.float64), axis, -1)
    blocks = v.reshape(v.shape[:-1] + (-1, 32))
    amax = np.abs(blocks).max(-1, keepdims=True)
    byte = np.maximum(np.where(amax > 0, np.frexp(amax)[1] - 1 + 127, 0) - down, 1)
    scale = np.exp2(byte - 127.0)
    codes = (blocks / scale).astype(np.float32).astype(dtype).astype(np.float64)
    return np.moveaxis((codes * scale).reshape(v.shape), -1, axis)


WIDE = False


def mx_kscale(k):
    if not WIDE:
        return np.ones(k)
    levels = np.array([10, -10, 5, -5, 0])
    if k % 512:
        return np.exp2(np.random.permutation(np.resize(levels, k // 32))).repeat(32)
    a = np.empty((k // 512, 16))
    for p in range(k // 512):
        a[p, :8] = np.random.permutation(np.resize(levels, 8))
        for g in range(8):
            far = levels[np.abs(levels - a[p, g]) >= 10]
            a[p, g + 8] = far[np.random.randint(len(far))]
    return np.exp2(a.ravel()).repeat(32)


def f64(x):
    return np.asarray(x).astype(np.float64)


def striped8(idx):
    return np.concatenate([v.reshape(-1, 16).T for v in idx]).astype(np.uint16)


def unstriped8(offs):
    return np.stack([offs[16 * g:16 * g + 16].T.reshape(-1) for g in range(8)]).astype(np.int64)


E2M1 = np.array([0.0, 0.5, 1.0, 1.5, 2.0, 3.0, 4.0, 6.0, -0.0, -0.5, -1.0, -1.5, -2.0, -3.0, -4.0, -6.0])


def pack_weight(w, fmt):
    k, n = w.shape
    w = f64(np.asarray(w, np.float32).astype(ml_dtypes.bfloat16)).reshape(k // 32, 32, n)
    amax = np.abs(w).max(1)
    if fmt == "e4m3":
        byte = np.frexp(amax)[1] - 1 + 127 - 7
    else:
        mant, ex = np.frexp(amax / 6.0)
        byte = np.where(mant > 0.5, ex, ex - 1) + 127
    byte = np.clip(np.where(amax > 0, byte, 1), 1, 254)
    scaled = (w * np.exp2(127.0 - byte)[:, None, :]).reshape(k, n).astype(np.float32)
    by_word = np.ascontiguousarray(scaled.reshape(k // 512, 128, 4, n).transpose(0, 1, 3, 2))
    if fmt == "e4m3":
        words = by_word.astype(ml_dtypes.float8_e4m3fn).view(np.uint8)
    else:
        c = by_word.astype(ml_dtypes.float4_e2m1fn).view(np.uint8) & 0xF
        words = (c[..., 0::2] | (c[..., 1::2] << 4)).reshape(k // 512, 128, 2 * n)
    return np.ascontiguousarray(words), np.ascontiguousarray(byte.astype(np.uint8).reshape(k // 512, 16, n))


def unpack_weight(words, scales, fmt):
    g, _, n = scales.shape
    words = np.ascontiguousarray(words).reshape(g, 128, n, -1)
    if fmt == "e4m3":
        vals = words.view(ml_dtypes.float8_e4m3fn).astype(np.float64)
    else:
        nib = np.empty((g, 128, n, 4), np.uint8)
        nib[..., 0::2] = words & 0xF
        nib[..., 1::2] = words >> 4
        vals = E2M1[nib]
    vals = vals * np.repeat(np.exp2(scales.astype(np.float64) - 127.0), 8, axis=1)[..., None]
    return vals.transpose(0, 1, 3, 2).reshape(g * 512, n)


def silu(v):
    return v / (1.0 + np.exp(-np.maximum(v, -700.0)))


K, L, M, T, S = 512, 512, 512, 2048, 1024


def setup_inputs():
    n = np.random.standard_normal
    s1 = mx_kscale(K)[:, None]
    s2 = mx_kscale(L)[:, None]
    p_w4 = pack_weight(n((K, M)) / np.sqrt(K) / s1, "e2m1")
    return {
        "xT": (n((K, T)) * s1).astype(np.float32),
        "w4_words": p_w4[0],
        "w4_scales": p_w4[1],
        "c": (n((L, S)) * s2).astype(np.float32),
        "u": (n((L, M)) / np.sqrt(L) / s2).astype(np.float32),
        "wgt": np.repeat(np.random.uniform(0.5, 2.0, (8, S)), 16, axis=0).astype(np.float32),
        "b": (0.3 * n(512)).astype(np.float32),
        "offs": striped8(np.stack([np.random.permutation(T)[:S] for _ in range(8)])),
    }


def reference(xT, w4_words, w4_scales, c, u, wgt, b, offs):
    idx = unstriped8(offs)
    group = np.arange(K) % 512 // 64
    xg = f64(wgt)[np.arange(K) // 4 % 128] * f64(xT)[np.arange(K)[:, None], idx[group]]
    xT_ = mxq(xg, 0, "e4m3")
    w4_ = unpack_weight(w4_words, w4_scales, "e2m1")
    c_ = mxq(f64(c), 0, "e4m3")
    u_ = mxq(f64(u), 0, "e4m3")
    y = w4_.T @ xT_ + u_.T @ c_
    return silu(y + f64(b)[:, None])

@@ -1,0 +1,194 @@
+from contextlib import ExitStack
+
+import concourse.mybir as mybir
+
+F32 = mybir.dt.float32
+BF16 = mybir.dt.bfloat16
+I32 = mybir.dt.int32
+U32 = mybir.dt.uint32
+U16 = mybir.dt.uint16
+U8 = mybir.dt.uint8
+E4M3X4 = mybir.dt.float8_e4m3fn_x4
+E2M1X4 = mybir.dt.float4_e2m1fn_x4
+MULT = mybir.AluOpType.mult
+SILU = mybir.ActivationFunctionType.Silu
+
+K, L, M, T, S = 512, 512, 512, 2048, 1024
+FLOPS = 2 * M * S * (K + L)
+
+P = 128
+PACK = 4
+HALF = 512
+QUART = 256
+NQ = S // QUART
+GROUP = 128
+MT = M // P
+
+
+def tile_list_hmix_silu_kernel(tc, xT, w4_words, w4_scales, c, u, wgt, b, offs, out):
+    nc = tc.nc
+    with ExitStack() as ctx:
+        keep = ctx.enter_context(tc.tile_pool(name="keep", bufs=1))
+        psum = ctx.enter_context(tc.psum_pool(name="psum", bufs=2))
+
+        offsets = keep.tile([P, S // 16], U16, name="offsets")
+        nc.sync.dma_start(offsets[:], offs)
+
+        x_planes = xT.rearrange("(p i) t -> i p t", i=PACK)
+        x_sb = []
+        w_sb = []
+        for h in range(2):
+            w_h = keep.tile([P, HALF], F32, name=f"wgt{h}")
+            w_sb.append(w_h)
+        for i in range(PACK):
+            x_i = keep.tile([P, T], F32, name=f"x{i}")
+            x_sb.append(x_i)
+
+        nc.sync.dma_start(x_sb[0][:], x_planes[0])
+        nc.sync.dma_start(w_sb[0][:], wgt[:, 0:HALF])
+        nc.sync.dma_start(w_sb[1][:], wgt[:, HALF:S])
+        for i in range(1, PACK):
+            nc.sync.dma_start(x_sb[i][:], x_planes[i])
+
+        w4s = keep.tile([P, M], U8, name="w4s", align_bytes=64)
+        nc.gpsimd.memset(w4s[:].bitcast(I32), 0)
+        for q in range(4):
+            nc.scalar.dma_start(w4s[32 * q : 32 * q + 4, :].bitcast(I32), w4_scales[0, 4 * q : 4 * q + 4, :].bitcast(I32))
+        bias = keep.tile([P, MT], F32, name="bias")
+        with nc.allow_non_contiguous_dma("bias: one value a partition"):
+            nc.scalar.dma_start(bias[:], b.rearrange("(m p) -> p m", p=P))
+
+        warm = keep.tile([P, 1], F32, name="warm")
+        nc.gpsimd.memset(warm[:], 0.0)
+        nc.scalar.activation(warm[:], warm[:], SILU)
+
+        u_rows = u.rearrange("(p i) n -> p i n", i=PACK)
+        c_rows = c.rearrange("(p i) s -> p i s", i=PACK)
+        u_sb = []
+        c_sb = []
+        for k in range(2):
+            u_k = keep.tile([P, PACK, QUART], F32, name=f"u{k}")
+            u_sb.append(u_k)
+        for q in range(NQ):
+            c_q = keep.tile([P, PACK, QUART], F32, name=f"c{q}")
+            c_sb.append(c_q)
+        w4 = keep.tile([P, 2 * M], U8, name="w4", align_bytes=64)
+
+        def load_u(k):
+            nc.sync.dma_start(u_sb[k][:], u_rows[:, :, k * QUART : (k + 1) * QUART])
+
+        def load_c(q):
+            nc.sync.dma_start(c_sb[q][:], c_rows[:, :, q * QUART : (q + 1) * QUART])
+
+        load_u(0)
+        load_c(0)
+        load_u(1)
+        nc.sync.dma_start(w4[:].bitcast(I32), w4_words[0].bitcast(I32))
+        load_c(1)
+        load_c(2)
+        load_c(3)
+
+        g = []
+        for h in range(2):
+            g_h = keep.tile([P, PACK, HALF], F32, name=f"g{h}")
+            g.append(g_h)
+        for i in range(PACK):
+            for h in range(2):
+                nc.vector.tensor_tensor(
+                    g[h][:, i, :],
+                    x_sb[i][:].indirect(offsets[:, h * (HALF // 16) : (h + 1) * (HALF // 16)]),
+                    w_sb[h][:],
+                    MULT,
+                )
+
+        ub = keep.tile([P, M, PACK], BF16, name="ub", align_bytes=64)
+        cb = []
+        xb = []
+        for q in range(NQ):
+            cb_q = keep.tile([P, QUART, PACK], BF16, name=f"cb{q}", align_bytes=64)
+            cb.append(cb_q)
+            xb_q = keep.tile([P, QUART, PACK], BF16, name=f"xb{q}", align_bytes=64)
+            xb.append(xb_q)
+
+        def interleave(eng, dst, src):
+            d = dst.rearrange("p (n r) i -> p n i r", r=4)
+            s = src.rearrange("p i (n r) -> p n i r", r=4)
+            if eng == "V":
+                nc.vector.tensor_copy(d, s)
+            else:
+                nc.scalar.copy(d, s)
+
+        def do_u(eng, k):
+            interleave(eng, ub[:, k * QUART : (k + 1) * QUART, :], u_sb[k][:])
+
+        def do_c(eng, q):
+            interleave(eng, cb[q][:], c_sb[q][:])
+
+        def do_x(eng, q):
+            lo = (q % 2) * QUART
+            interleave(eng, xb[q][:], g[q // 2][:, :, lo : lo + QUART])
+
+        def quantize(name, src, cols):
+            words = keep.tile([P, cols], U32, name=f"{name}_w", align_bytes=64)
+            scales = keep.tile([P, cols], U8, name=f"{name}_s", align_bytes=64)
+            nc.vector.quantize_mx(out=words[:].bitcast(E4M3X4), scales=scales[:], in_=src.rearrange("p n i -> p (n i)"))
+            return words, scales
+
+        ob = []
+        for q in range(NQ):
+            ob_q = keep.tile([P, MT, QUART], F32, name=f"ob{q}")
+            ob.append(ob_q)
+        out_rows = out.rearrange("(m p) s -> p m s", p=P)
+
+        def product(q, uq, xq, cq):
+            for m in range(MT):
+                acc = psum.tile([P, QUART], F32, name=f"acc{m}")
+                for n0 in range(0, QUART, GROUP):
+                    cols = slice(n0, n0 + GROUP)
+                    nc.tensor.matmul_mx(
+                        out=acc[:, cols],
+                        lhsT=w4[:, 2 * P * m : 2 * P * (m + 1)].bitcast(E2M1X4),
+                        lhsT_scale=w4s[:, P * m : P * (m + 1)],
+                        rhs=xq[0][:, cols].bitcast(E4M3X4),
+                        rhs_scale=xq[1][:, cols],
+                        start=True,
+                        stop=False,
+                    )
+                    nc.tensor.matmul_mx(
+                        out=acc[:, cols],
+                        lhsT=uq[0][:, P * m : P * (m + 1)].bitcast(E4M3X4),
+                        lhsT_scale=uq[1][:, P * m : P * (m + 1)],
+                        rhs=cq[0][:, cols].bitcast(E4M3X4),
+                        rhs_scale=cq[1][:, cols],
+                        start=False,
+                        stop=True,
+                    )
+                nc.scalar.activation(ob[q][:, m, :], acc[:], SILU, bias=bias[:, m : m + 1])
+                if m % 2 == 1:
+                    nc.sync.dma_start(
+                        out_rows[:, m - 1 : m + 1, q * QUART : (q + 1) * QUART], ob[q][:, m - 1 : m + 1, :]
+                    )
+
+        do_u("S", 0)
+        do_c("S", 0)
+        do_x("V", 1)
+        do_u("V", 1)
+        do_x("S", 0)
+        cq0 = quantize("cq0", cb[0][:], QUART)
+        uq = quantize("uq", ub[:], M)
+        xq0 = quantize("xq0", xb[0][:], QUART)
+        do_x("S", 2)
+        do_c("V", 1)
+        product(0, uq, xq0, cq0)
+        xq1 = quantize("xq1", xb[1][:], QUART)
+        cq1 = quantize("cq1", cb[1][:], QUART)
+        product(1, uq, xq1, cq1)
+        do_c("V", 2)
+        xq2 = quantize("xq2", xb[2][:], QUART)
+        cq2 = quantize("cq2", cb[2][:], QUART)
+        product(2, uq, xq2, cq2)
+        do_x("V", 3)
+        do_c("V", 3)
+        xq3 = quantize("xq3", xb[3][:], QUART)
+        cq3 = quantize("cq3", cb[3][:], QUART)
+        product(3, uq, xq3, cq3)

@@ -50,13 +50,17 @@ def tile_list_hmix_silu_kernel(tc, xT, w4_words, w4_scales, c, u, wgt, b, offs, 
         for i in range(1, PACK):
             nc.sync.dma_start(x_sb[i][:], x_planes[i])
 
+        b_rows = keep.tile([P, 32], F32, name="b_rows", align_bytes=64)
+        bias = keep.tile([P, 32], F32, name="bias", align_bytes=64)
         w4s = keep.tile([P, M], U8, name="w4s", align_bytes=64)
+        nc.gpsimd.memset(b_rows[:], 0.0)
         nc.gpsimd.memset(w4s[:].bitcast(I32), 0)
+        b_blocks = b.rearrange("(m k j) -> m k j", m=MT, k=4)
+        for m in range(MT):
+            nc.sync.dma_start(b_rows[m:P:32, :], b_blocks[m])
+
         for q in range(4):
             nc.scalar.dma_start(w4s[32 * q : 32 * q + 4, :].bitcast(I32), w4_scales[0, 4 * q : 4 * q + 4, :].bitcast(I32))
-        bias = keep.tile([P, MT], F32, name="bias")
-        with nc.allow_non_contiguous_dma("bias: one value a partition"):
-            nc.scalar.dma_start(bias[:], b.rearrange("(m p) -> p m", p=P))
 
         warm = keep.tile([P, 1], F32, name="warm")
         nc.gpsimd.memset(warm[:], 0.0)
@@ -64,8 +68,8 @@ def tile_list_hmix_silu_kernel(tc, xT, w4_words, w4_scales, c, u, wgt, b, offs, 
 
         u_rows = u.rearrange("(p i) n -> p i n", i=PACK)
         c_rows = c.rearrange("(p i) s -> p i s", i=PACK)
-        u_sb = []
         c_sb = []
+        u_sb = []
         for k in range(2):
             u_k = keep.tile([P, PACK, QUART], F32, name=f"u{k}")
             u_sb.append(u_k)
@@ -74,11 +78,11 @@ def tile_list_hmix_silu_kernel(tc, xT, w4_words, w4_scales, c, u, wgt, b, offs, 
             c_sb.append(c_q)
         w4 = keep.tile([P, 2 * M], U8, name="w4", align_bytes=64)
 
-        def load_u(k):
-            nc.sync.dma_start(u_sb[k][:], u_rows[:, :, k * QUART : (k + 1) * QUART])
-
         def load_c(q):
             nc.sync.dma_start(c_sb[q][:], c_rows[:, :, q * QUART : (q + 1) * QUART])
+
+        def load_u(k):
+            nc.sync.dma_start(u_sb[k][:], u_rows[:, :, k * QUART : (k + 1) * QUART])
 
         load_u(0)
         load_c(0)
@@ -101,15 +105,6 @@ def tile_list_hmix_silu_kernel(tc, xT, w4_words, w4_scales, c, u, wgt, b, offs, 
                     MULT,
                 )
 
-        ub = keep.tile([P, M, PACK], BF16, name="ub", align_bytes=64)
-        cb = []
-        xb = []
-        for q in range(NQ):
-            cb_q = keep.tile([P, QUART, PACK], BF16, name=f"cb{q}", align_bytes=64)
-            cb.append(cb_q)
-            xb_q = keep.tile([P, QUART, PACK], BF16, name=f"xb{q}", align_bytes=64)
-            xb.append(xb_q)
-
         def interleave(eng, dst, src):
             d = dst.rearrange("p (n r) i -> p n i r", r=4)
             s = src.rearrange("p i (n r) -> p n i r", r=4)
@@ -118,15 +113,22 @@ def tile_list_hmix_silu_kernel(tc, xT, w4_words, w4_scales, c, u, wgt, b, offs, 
             else:
                 nc.scalar.copy(d, s)
 
-        def do_u(eng, k):
+        def stage(slot, name, cols):
+            return keep.tile([P, cols, PACK], BF16, name=name, tag=f"stage{slot}", align_bytes=64)
+
+        def do_u(eng, ub, k):
             interleave(eng, ub[:, k * QUART : (k + 1) * QUART, :], u_sb[k][:])
 
-        def do_c(eng, q):
-            interleave(eng, cb[q][:], c_sb[q][:])
+        def do_c(eng, q, slot):
+            cb = stage(slot, f"cb{q}", QUART)
+            interleave(eng, cb[:], c_sb[q][:])
+            return cb
 
-        def do_x(eng, q):
+        def do_x(eng, q, slot):
             lo = (q % 2) * QUART
-            interleave(eng, xb[q][:], g[q // 2][:, :, lo : lo + QUART])
+            xb = stage(slot, f"xb{q}", QUART)
+            interleave(eng, xb[:], g[q // 2][:, :, lo : lo + QUART])
+            return xb
 
         def quantize(name, src, cols):
             words = keep.tile([P, cols], U32, name=f"{name}_w", align_bytes=64)
@@ -142,53 +144,60 @@ def tile_list_hmix_silu_kernel(tc, xT, w4_words, w4_scales, c, u, wgt, b, offs, 
 
         def product(q, uq, xq, cq):
             for m in range(MT):
-                acc = psum.tile([P, QUART], F32, name=f"acc{m}")
+                acc = psum.tile([P, QUART], F32, name=f"acc{m}", tag=f"acc{m}")
                 for n0 in range(0, QUART, GROUP):
                     cols = slice(n0, n0 + GROUP)
-                    nc.tensor.matmul_mx(
-                        out=acc[:, cols],
-                        lhsT=w4[:, 2 * P * m : 2 * P * (m + 1)].bitcast(E2M1X4),
-                        lhsT_scale=w4s[:, P * m : P * (m + 1)],
-                        rhs=xq[0][:, cols].bitcast(E4M3X4),
-                        rhs_scale=xq[1][:, cols],
-                        start=True,
-                        stop=False,
-                    )
                     nc.tensor.matmul_mx(
                         out=acc[:, cols],
                         lhsT=uq[0][:, P * m : P * (m + 1)].bitcast(E4M3X4),
                         lhsT_scale=uq[1][:, P * m : P * (m + 1)],
                         rhs=cq[0][:, cols].bitcast(E4M3X4),
                         rhs_scale=cq[1][:, cols],
+                        start=True,
+                        stop=False,
+                    )
+                    nc.tensor.matmul_mx(
+                        out=acc[:, cols],
+                        lhsT=w4[:, 2 * P * m : 2 * P * (m + 1)].bitcast(E2M1X4),
+                        lhsT_scale=w4s[:, P * m : P * (m + 1)],
+                        rhs=xq[0][:, cols].bitcast(E4M3X4),
+                        rhs_scale=xq[1][:, cols],
                         start=False,
                         stop=True,
                     )
                 nc.scalar.activation(ob[q][:, m, :], acc[:], SILU, bias=bias[:, m : m + 1])
-                if m % 2 == 1:
+                if q == NQ - 1:
+                    nc.sync.dma_start(out_rows[:, m, q * QUART : (q + 1) * QUART], ob[q][:, m, :])
+                elif m % 2 == 1:
                     nc.sync.dma_start(
                         out_rows[:, m - 1 : m + 1, q * QUART : (q + 1) * QUART], ob[q][:, m - 1 : m + 1, :]
                     )
 
-        do_u("S", 0)
-        do_c("S", 0)
-        do_x("V", 1)
-        do_u("V", 1)
-        do_x("S", 0)
-        cq0 = quantize("cq0", cb[0][:], QUART)
+        def q_of(name, t):
+            return quantize(name, t[:], QUART)
+
+        ub = stage(0, "ub", M)
+        do_u("S", ub, 0)
+        cb = do_c("S", 0, 1)
+        xb = do_x("V", 0, 2)
+        do_u("S", ub, 1)
+        cq = q_of("cq0", cb)
+        xq = q_of("xq0", xb)
         uq = quantize("uq", ub[:], M)
-        xq0 = quantize("xq0", xb[0][:], QUART)
-        do_x("S", 2)
-        do_c("V", 1)
-        product(0, uq, xq0, cq0)
-        xq1 = quantize("xq1", xb[1][:], QUART)
-        cq1 = quantize("cq1", cb[1][:], QUART)
-        product(1, uq, xq1, cq1)
-        do_c("V", 2)
-        xq2 = quantize("xq2", xb[2][:], QUART)
-        cq2 = quantize("cq2", cb[2][:], QUART)
-        product(2, uq, xq2, cq2)
-        do_x("V", 3)
-        do_c("V", 3)
-        xq3 = quantize("xq3", xb[3][:], QUART)
-        cq3 = quantize("cq3", cb[3][:], QUART)
-        product(3, uq, xq3, cq3)
+        nc.vector.transpose(bias[:], b_rows[:])
+        xb2 = do_x("S", 2, 1)
+        xb = do_x("V", 1, 0)
+        cb = do_c("V", 1, 3)
+        product(0, uq, xq, cq)
+        xq = q_of("xq1", xb)
+        cq = q_of("cq1", cb)
+        product(1, uq, xq, cq)
+        cb = do_c("V", 2, 2)
+        xq = q_of("xq2", xb2)
+        cq = q_of("cq2", cb)
+        product(2, uq, xq, cq)
+        xb = do_x("V", 3, 0)
+        cb = do_c("V", 3, 3)
+        xq = q_of("xq3", xb)
+        cq = q_of("cq3", cb)
+        product(3, uq, xq, cq)

@@ -142,30 +142,40 @@ def tile_list_hmix_silu_kernel(tc, xT, w4_words, w4_scales, c, u, wgt, b, offs, 
             ob.append(ob_q)
         out_rows = out.rearrange("(m p) s -> p m s", p=P)
 
+        def x_pass(acc, m, cols, xq):
+            nc.tensor.matmul_mx(
+                out=acc[:, cols],
+                lhsT=w4[:, 2 * P * m : 2 * P * (m + 1)].bitcast(E2M1X4),
+                lhsT_scale=w4s[:, P * m : P * (m + 1)],
+                rhs=xq[0][:, cols].bitcast(E4M3X4),
+                rhs_scale=xq[1][:, cols],
+                start=True,
+                stop=False,
+            )
+
+        def c_pass(acc, m, cols, uq, cq):
+            nc.tensor.matmul_mx(
+                out=acc[:, cols],
+                lhsT=uq[0][:, P * m : P * (m + 1)].bitcast(E4M3X4),
+                lhsT_scale=uq[1][:, P * m : P * (m + 1)],
+                rhs=cq[0][:, cols].bitcast(E4M3X4),
+                rhs_scale=cq[1][:, cols],
+                start=False,
+                stop=True,
+            )
+
         def product(q, uq, xq, cq):
+            low, high = slice(0, GROUP), slice(GROUP, QUART)
+            accs = []
             for m in range(MT):
                 acc = psum.tile([P, QUART], F32, name=f"acc{m}", tag=f"acc{m}")
-                for n0 in range(0, QUART, GROUP):
-                    cols = slice(n0, n0 + GROUP)
-                    nc.tensor.matmul_mx(
-                        out=acc[:, cols],
-                        lhsT=uq[0][:, P * m : P * (m + 1)].bitcast(E4M3X4),
-                        lhsT_scale=uq[1][:, P * m : P * (m + 1)],
-                        rhs=cq[0][:, cols].bitcast(E4M3X4),
-                        rhs_scale=cq[1][:, cols],
-                        start=True,
-                        stop=False,
-                    )
-                    nc.tensor.matmul_mx(
-                        out=acc[:, cols],
-                        lhsT=w4[:, 2 * P * m : 2 * P * (m + 1)].bitcast(E2M1X4),
-                        lhsT_scale=w4s[:, P * m : P * (m + 1)],
-                        rhs=xq[0][:, cols].bitcast(E4M3X4),
-                        rhs_scale=xq[1][:, cols],
-                        start=False,
-                        stop=True,
-                    )
-                nc.scalar.activation(ob[q][:, m, :], acc[:], SILU, bias=bias[:, m : m + 1])
+                accs.append(acc)
+                x_pass(acc, m, low, xq)
+            for m in range(MT):
+                c_pass(accs[m], m, low, uq, cq)
+                x_pass(accs[m], m, high, xq)
+                c_pass(accs[m], m, high, uq, cq)
+                nc.scalar.activation(ob[q][:, m, :], accs[m][:], SILU, bias=bias[:, m : m + 1])
                 if q == NQ - 1:
                     nc.sync.dma_start(out_rows[:, m, q * QUART : (q + 1) * QUART], ob[q][:, m, :])
                 elif m % 2 == 1:

@@ -190,7 +190,7 @@ def tile_list_hmix_silu_kernel(tc, xT, w4_words, w4_scales, c, u, wgt, b, offs, 
         do_u("S", ub, 0)
         cb = do_c("S", 0, 1)
         xb = do_x("V", 0, 2)
-        do_u("S", ub, 1)
+        do_u("V", ub, 1)
         cq = q_of("cq0", cb)
         xq = q_of("xq0", xb)
         uq = quantize("uq", ub[:], M)

from contextlib import ExitStack

import concourse.mybir as mybir

F32 = mybir.dt.float32
BF16 = mybir.dt.bfloat16
I32 = mybir.dt.int32
U32 = mybir.dt.uint32
U16 = mybir.dt.uint16
U8 = mybir.dt.uint8
E4M3X4 = mybir.dt.float8_e4m3fn_x4
E2M1X4 = mybir.dt.float4_e2m1fn_x4
MULT = mybir.AluOpType.mult
SILU = mybir.ActivationFunctionType.Silu

K, L, M, T, S = 512, 512, 512, 2048, 1024
FLOPS = 2 * M * S * (K + L)

P = 128
PACK = 4
HALF = 512
QUART = 256
NQ = S // QUART
GROUP = 128
MT = M // P


def tile_list_hmix_silu_kernel(tc, xT, w4_words, w4_scales, c, u, wgt, b, offs, out):
    nc = tc.nc
    with ExitStack() as ctx:
        keep = ctx.enter_context(tc.tile_pool(name="keep", bufs=1))
        psum = ctx.enter_context(tc.psum_pool(name="psum", bufs=2))

        offsets = keep.tile([P, S // 16], U16, name="offsets")
        nc.sync.dma_start(offsets[:], offs)

        x_planes = xT.rearrange("(p i) t -> i p t", i=PACK)
        x_sb = []
        w_sb = []
        for h in range(2):
            w_h = keep.tile([P, HALF], F32, name=f"wgt{h}")
            w_sb.append(w_h)
        for i in range(PACK):
            x_i = keep.tile([P, T], F32, name=f"x{i}")
            x_sb.append(x_i)

        nc.sync.dma_start(x_sb[0][:], x_planes[0])
        nc.sync.dma_start(w_sb[0][:], wgt[:, 0:HALF])
        nc.sync.dma_start(w_sb[1][:], wgt[:, HALF:S])
        for i in range(1, PACK):
            nc.sync.dma_start(x_sb[i][:], x_planes[i])

        b_rows = keep.tile([P, 32], F32, name="b_rows", align_bytes=64)
        bias = keep.tile([P, 32], F32, name="bias", align_bytes=64)
        w4s = keep.tile([P, M], U8, name="w4s", align_bytes=64)
        nc.gpsimd.memset(b_rows[:], 0.0)
        nc.gpsimd.memset(w4s[:].bitcast(I32), 0)
        b_blocks = b.rearrange("(m k j) -> m k j", m=MT, k=4)
        for m in range(MT):
            nc.sync.dma_start(b_rows[m:P:32, :], b_blocks[m])

        for q in range(4):
            nc.scalar.dma_start(w4s[32 * q : 32 * q + 4, :].bitcast(I32), w4_scales[0, 4 * q : 4 * q + 4, :].bitcast(I32))

        warm = keep.tile([P, 1], F32, name="warm")
        nc.gpsimd.memset(warm[:], 0.0)
        nc.scalar.activation(warm[:], warm[:], SILU)

        u_rows = u.rearrange("(p i) n -> p i n", i=PACK)
        c_rows = c.rearrange("(p i) s -> p i s", i=PACK)
        c_sb = []
        u_sb = []
        for k in range(2):
            u_k = keep.tile([P, PACK, QUART], F32, name=f"u{k}")
            u_sb.append(u_k)
        for q in range(NQ):
            c_q = keep.tile([P, PACK, QUART], F32, name=f"c{q}")
            c_sb.append(c_q)
        w4 = keep.tile([P, 2 * M], U8, name="w4", align_bytes=64)

        def load_c(q):
            nc.sync.dma_start(c_sb[q][:], c_rows[:, :, q * QUART : (q + 1) * QUART])

        def load_u(k):
            nc.sync.dma_start(u_sb[k][:], u_rows[:, :, k * QUART : (k + 1) * QUART])

        load_u(0)
        load_c(0)
        load_u(1)
        nc.sync.dma_start(w4[:].bitcast(I32), w4_words[0].bitcast(I32))
        load_c(1)
        load_c(2)
        load_c(3)

        g = []
        for h in range(2):
            g_h = keep.tile([P, PACK, HALF], F32, name=f"g{h}")
            g.append(g_h)
        for i in range(PACK):
            for h in range(2):
                nc.vector.tensor_tensor(
                    g[h][:, i, :],
                    x_sb[i][:].indirect(offsets[:, h * (HALF // 16) : (h + 1) * (HALF // 16)]),
                    w_sb[h][:],
                    MULT,
                )

        def interleave(eng, dst, src):
            d = dst.rearrange("p (n r) i -> p n i r", r=4)
            s = src.rearrange("p i (n r) -> p n i r", r=4)
            if eng == "V":
                nc.vector.tensor_copy(d, s)
            else:
                nc.scalar.copy(d, s)

        def stage(slot, name, cols):
            return keep.tile([P, cols, PACK], BF16, name=name, tag=f"stage{slot}", align_bytes=64)

        def do_u(eng, ub, k):
            interleave(eng, ub[:, k * QUART : (k + 1) * QUART, :], u_sb[k][:])

        def do_c(eng, q, slot):
            cb = stage(slot, f"cb{q}", QUART)
            interleave(eng, cb[:], c_sb[q][:])
            return cb

        def do_x(eng, q, slot):
            lo = (q % 2) * QUART
            xb = stage(slot, f"xb{q}", QUART)
            interleave(eng, xb[:], g[q // 2][:, :, lo : lo + QUART])
            return xb

        def quantize(name, src, cols):
            words = keep.tile([P, cols], U32, name=f"{name}_w", align_bytes=64)
            scales = keep.tile([P, cols], U8, name=f"{name}_s", align_bytes=64)
            nc.vector.quantize_mx(out=words[:].bitcast(E4M3X4), scales=scales[:], in_=src.rearrange("p n i -> p (n i)"))
            return words, scales

        ob = []
        for q in range(NQ):
            ob_q = keep.tile([P, MT, QUART], F32, name=f"ob{q}")
            ob.append(ob_q)
        out_rows = out.rearrange("(m p) s -> p m s", p=P)

        def x_pass(acc, m, cols, xq):
            nc.tensor.matmul_mx(
                out=acc[:, cols],
                lhsT=w4[:, 2 * P * m : 2 * P * (m + 1)].bitcast(E2M1X4),
                lhsT_scale=w4s[:, P * m : P * (m + 1)],
                rhs=xq[0][:, cols].bitcast(E4M3X4),
                rhs_scale=xq[1][:, cols],
                start=True,
                stop=False,
            )

        def c_pass(acc, m, cols, uq, cq):
            nc.tensor.matmul_mx(
                out=acc[:, cols],
                lhsT=uq[0][:, P * m : P * (m + 1)].bitcast(E4M3X4),
                lhsT_scale=uq[1][:, P * m : P * (m + 1)],
                rhs=cq[0][:, cols].bitcast(E4M3X4),
                rhs_scale=cq[1][:, cols],
                start=False,
                stop=True,
            )

        def product(q, uq, xq, cq):
            low, high = slice(0, GROUP), slice(GROUP, QUART)
            accs = []
            for m in range(MT):
                acc = psum.tile([P, QUART], F32, name=f"acc{m}", tag=f"acc{m}")
                accs.append(acc)
                x_pass(acc, m, low, xq)
            for m in range(MT):
                c_pass(accs[m], m, low, uq, cq)
                x_pass(accs[m], m, high, xq)
                c_pass(accs[m], m, high, uq, cq)
                nc.scalar.activation(ob[q][:, m, :], accs[m][:], SILU, bias=bias[:, m : m + 1])
                if q == NQ - 1:
                    nc.sync.dma_start(out_rows[:, m, q * QUART : (q + 1) * QUART], ob[q][:, m, :])
                elif m % 2 == 1:
                    nc.sync.dma_start(
                        out_rows[:, m - 1 : m + 1, q * QUART : (q + 1) * QUART], ob[q][:, m - 1 : m + 1, :]
                    )

        def q_of(name, t):
            return quantize(name, t[:], QUART)

        ub = stage(0, "ub", M)
        do_u("S", ub, 0)
        cb = do_c("S", 0, 1)
        xb = do_x("V", 0, 2)
        do_u("V", ub, 1)
        cq = q_of("cq0", cb)
        xq = q_of("xq0", xb)
        uq = quantize("uq", ub[:], M)
        nc.vector.transpose(bias[:], b_rows[:])
        xb2 = do_x("S", 2, 1)
        xb = do_x("V", 1, 0)
        cb = do_c("V", 1, 3)
        product(0, uq, xq, cq)
        xq = q_of("xq1", xb)
        cq = q_of("cq1", cb)
        product(1, uq, xq, cq)
        cb = do_c("V", 2, 2)
        xq = q_of("xq2", xb2)
        cq = q_of("cq2", cb)
        product(2, uq, xq, cq)
        xb = do_x("V", 3, 0)
        cb = do_c("V", 3, 3)
        xq = q_of("xq3", xb)
        cq = q_of("cq3", cb)
        product(3, uq, xq, cq)
